import numpy as np
import ml_dtypes


def mxq(x, axis, fmt="e4m3"):
    dtype, down = {"e4m3": (ml_dtypes.float8_e4m3fn, 7), "e5m2": (ml_dtypes.float8_e5m2, 14)}[fmt]
    v = np.moveaxis(np.asarray(x, np.float32).astype(ml_dtypes.bfloat16).astype(np.float64), axis, -1)
    blocks = v.reshape(v.shape[:-1] + (-1, 32))
    amax = np.abs(blocks).max(-1, keepdims=True)
    byte = np.maximum(np.where(amax > 0, np.frexp(amax)[1] - 1 + 127, 0) - down, 1)
    scale = np.exp2(byte - 127.0)
    codes = (blocks / scale).astype(np.float32).astype(dtype).astype(np.float64)
    return np.moveaxis((codes * scale).reshape(v.shape), -1, axis)


WIDE = False


def mx_kscale(k):
    if not WIDE:
        return np.ones(k)
    levels = np.array([10, -10, 5, -5, 0])
    if k % 512:
        return np.exp2(np.random.permutation(np.resize(levels, k // 32))).repeat(32)
    a = np.empty((k // 512, 16))
    for p in range(k // 512):
        a[p, :8] = np.random.permutation(np.resize(levels, 8))
        for g in range(8):
            far = levels[np.abs(levels - a[p, g]) >= 10]
            a[p, g + 8] = far[np.random.randint(len(far))]
    return np.exp2(a.ravel()).repeat(32)


def f64(x):
    return np.asarray(x).astype(np.float64)


def striped8(idx):
    return np.asarray(idx).reshape(8, -1, 16).transpose(0, 2, 1).reshape(128, -1).astype(np.uint16)


def unstriped8(offs):
    return offs.reshape(8, 16, -1).transpose(0, 2, 1).reshape(8, -1).astype(np.int64)


def pick8(x, idx, run):
    r = np.arange(len(x))
    return x[r[:, None], idx[r % (8 * run) // run]]


E2M1 = np.array([0.0, 0.5, 1.0, 1.5, 2.0, 3.0, 4.0, 6.0, -0.0, -0.5, -1.0, -1.5, -2.0, -3.0, -4.0, -6.0])


def pack_weight(w, fmt):
    k, n = w.shape
    w = f64(np.asarray(w, np.float32).astype(ml_dtypes.bfloat16)).reshape(k // 32, 32, n)
    amax = np.abs(w).max(1)
    if fmt == "e4m3":
        byte = np.frexp(amax)[1] - 1 + 127 - 7
    else:
        mant, ex = np.frexp(amax / 6.0)
        byte = np.where(mant > 0.5, ex, ex - 1) + 127
    byte = np.clip(np.where(amax > 0, byte, 1), 1, 254)
    scaled = (w * np.exp2(127.0 - byte)[:, None, :]).reshape(k, n).astype(np.float32)
    by_word = np.ascontiguousarray(scaled.reshape(k // 512, 128, 4, n).transpose(0, 1, 3, 2))
    if fmt == "e4m3":
        words = by_word.astype(ml_dtypes.float8_e4m3fn).view(np.uint8)
    else:
        c = by_word.astype(ml_dtypes.float4_e2m1fn).view(np.uint8) & 0xF
        words = (c[..., 0::2] | (c[..., 1::2] << 4)).reshape(k // 512, 128, 2 * n)
    return np.ascontiguousarray(words), np.ascontiguousarray(byte.astype(np.uint8).reshape(k // 512, 16, n))


def unpack_weight(words, scales, fmt):
    g, _, n = scales.shape
    words = np.ascontiguousarray(words).reshape(g, 128, n, -1)
    if fmt == "e4m3":
        vals = words.view(ml_dtypes.float8_e4m3fn).astype(np.float64)
    else:
        nib = np.empty((g, 128, n, 4), np.uint8)
        nib[..., 0::2] = words & 0xF
        nib[..., 1::2] = words >> 4
        vals = E2M1[nib]
    vals = vals * np.repeat(np.exp2(scales.astype(np.float64) - 127.0), 8, axis=1)[..., None]
    return vals.transpose(0, 1, 3, 2).reshape(g * 512, n)


D, T, U, X, I, Q = 512, 1024, 1024, 1024, 512, 128


def setup_inputs():
    n = np.random.standard_normal
    idx = np.stack([np.random.permutation(T)[:I] for _ in range(8)])
    idx2 = np.stack([np.random.permutation(U)[:I] for _ in range(8)])
    idx3 = np.stack([np.random.permutation(U)[:I] for _ in range(8)])
    idx4 = np.stack([np.random.permutation(X)[:I] for _ in range(8)])
    idx5 = np.stack([np.random.permutation(X)[:I] for _ in range(8)])
    fd = mx_kscale(D)
    keysp = pack_weight(n((D, T)) / fd[:, None], "e2m1")
    notesp = pack_weight(n((D, U)) / fd[:, None], "e4m3")
    usersp = pack_weight(n((D, X)) / fd[:, None], "e2m1")
    return {
        "query": (n((D, Q)) * 1.0 / np.sqrt(D) * fd[:, None]).astype(np.float32),
        "keys_words": keysp[0],
        "keys_scales": keysp[1],
        "notes_words": notesp[0],
        "notes_scales": notesp[1],
        "users_words": usersp[0],
        "users_scales": usersp[1],
        "offs": striped8(idx),
        "offs2": striped8(idx2),
        "offs3": striped8(idx3),
        "offs4": striped8(idx4),
        "offs5": striped8(idx5),
    }


def reference(query, keys_words, keys_scales, notes_words, notes_scales, users_words, users_scales, offs, offs2, offs3, offs4, offs5):
    idx = unstriped8(offs)
    idx2 = unstriped8(offs2)
    idx3 = unstriped8(offs3)
    idx4 = unstriped8(offs4)
    idx5 = unstriped8(offs5)
    keysu = unpack_weight(keys_words, keys_scales, "e2m1")
    notesu = unpack_weight(notes_words, notes_scales, "e4m3")
    usersu = unpack_weight(users_words, users_scales, "e2m1")
    queryq = mxq(f64(query), 0, "e4m3")
    a = queryq.T @ keysu
    b = queryq.T @ notesu
    c0 = queryq.T @ usersu
    f1 = np.zeros((Q, U))
    f1[np.arange(Q)[:, None], idx2[np.arange(Q) % 128 // 16]] = pick8(a, idx, 16)
    cc = b + f1
    f2 = np.zeros((Q, X))
    f2[np.arange(Q)[:, None], idx4[np.arange(Q) % 128 // 16]] = pick8(cc, idx3, 16)
    dd = c0 + f2
    y = pick8(dd, idx5, 16)
    return y

@@ -1,0 +1,119 @@
+from contextlib import ExitStack
+
+import concourse.mybir as mybir
+
+D, T, I, Q = 512, 1024, 512, 128
+FLOPS = 3 * 2 * D * T * Q
+
+F32 = mybir.dt.float32
+BF16 = mybir.dt.bfloat16
+I32 = mybir.dt.int32
+U32 = mybir.dt.uint32
+U16 = mybir.dt.uint16
+U8 = mybir.dt.uint8
+FP8X4 = mybir.dt.float8_e4m3fn_x4
+FP4X4 = mybir.dt.float4_e2m1fn_x4
+COPY = mybir.ActivationFunctionType.Copy
+ADD = mybir.AluOpType.add
+
+P = 128
+BANK = 512
+HALF = I // 2
+
+
+def tile_attend_relaythree_three_kernel(
+    tc, query, keys_words, keys_scales, notes_words, notes_scales, users_words, users_scales,
+    offs, offs2, offs3, offs4, offs5, out,
+):
+    nc = tc.nc
+    with ExitStack() as ctx:
+        sb = ctx.enter_context(tc.tile_pool(name="sb", bufs=1))
+        ps = ctx.enter_context(tc.psum_pool(name="ps", bufs=1))
+
+        def load_list(src, name):
+            lists = sb.tile([P, I // 16], U16, name=name)
+            nc.sync.dma_start(lists[:], src)
+            return lists
+
+        def load_words(src, nbytes, name):
+            words = sb.tile([P, nbytes], U8, name=name, align_bytes=64)
+            nc.sync.dma_start(words[:].bitcast(I32), src.bitcast(I32))
+            return words
+
+        def load_scales(src, name):
+            plane = sb.tile([P, T], U8, name=name, align_bytes=64)
+            for g in range(4):
+                nc.sync.dma_start(plane[32 * g : 32 * g + 4, :].bitcast(I32), src[0, 4 * g : 4 * g + 4, :].bitcast(I32))
+            return plane
+
+        q_raw = sb.tile([P, 4, Q], F32, name="q_raw")
+        nc.sync.dma_start(q_raw[:], query.rearrange("(p j) q -> p j q", j=4))
+        k_plane = load_scales(keys_scales, "k_plane")
+        k_words = load_words(keys_words[0], 2 * T, "k_words")
+        l1 = load_list(offs, "l1")
+        l2 = load_list(offs2, "l2")
+        n_plane = load_scales(notes_scales, "n_plane")
+        n_words = load_words(notes_words[0].rearrange("p n t -> p (n t)"), 4 * T, "n_words")
+        l3 = load_list(offs3, "l3")
+        l4 = load_list(offs4, "l4")
+        u_plane = load_scales(users_scales, "u_plane")
+        u_words = load_words(users_words[0], 2 * T, "u_words")
+        l5 = load_list(offs5, "l5")
+
+        f1 = sb.tile([P, T], F32, name="f1")
+        f2 = sb.tile([P, T], F32, name="f2")
+        nc.vector.memset(f1[:], 0.0)
+        nc.vector.memset(f2[:], 0.0)
+
+        q_bf = sb.tile([P, Q, 4], BF16, name="q_bf", align_bytes=64)
+        nc.vector.tensor_copy(
+            q_bf[:].rearrange("p (c i) t -> p c t i", i=4),
+            q_raw[:].rearrange("p t (c i) -> p c t i", i=4),
+        )
+        q_codes = sb.tile([P, Q], U32, name="q_codes", align_bytes=64)
+        q_plane = sb.tile([P, Q], U8, name="q_plane", align_bytes=64)
+        nc.vector.quantize_mx(q_codes[:].bitcast(FP8X4), q_plane[:], q_bf[:].rearrange("p c t -> p (c t)"))
+
+        def scores(words, plane, dtype, per_col, c0, n, tag):
+            acc = ps.tile([P, n], F32, name=tag)
+            nc.tensor.matmul_mx(
+                acc[:],
+                lhsT=q_codes[:].bitcast(FP8X4),
+                lhsT_scale=q_plane[:],
+                rhs=words[:, per_col * c0 : per_col * (c0 + n)].bitcast(dtype),
+                rhs_scale=plane[:, c0 : c0 + n],
+                start=True,
+                stop=True,
+            )
+            return acc
+
+        a = sb.tile([P, T], F32, name="a")
+        for j in range(4):
+            acc = scores(k_words, k_plane, FP4X4, 2, 256 * j, 256, "a%d" % j)
+            if j % 2 == 0:
+                nc.scalar.activation(a[:, 256 * j : 256 * (j + 1)], acc[:], COPY)
+            else:
+                nc.vector.tensor_copy(a[:, 256 * j : 256 * (j + 1)], acc[:])
+        b = [scores(n_words, n_plane, FP8X4, 4, BANK * j, BANK, "b%d" % j) for j in range(2)]
+        c = [scores(u_words, u_plane, FP4X4, 2, BANK * j, BANK, "c%d" % j) for j in range(2)]
+
+        def look_up(window, lists, name):
+            picked = sb.tile([P, I], F32, name=name)
+            nc.vector.tensor_copy(picked[:, :HALF], window[:].indirect(lists[:, : HALF // 16]))
+            nc.scalar.activation(picked[:, HALF:], window[:].indirect(lists[:, HALF // 16 :]), COPY)
+            return picked
+
+        def relay(window, pick, place, fresh, banks, name):
+            picked = look_up(window, pick, name + "_picked")
+            nc.vector.tensor_copy(fresh[:].indirect(place[:]), picked[:])
+            total = sb.tile([P, T], F32, name=name)
+            for j in range(2):
+                cols = slice(BANK * j, BANK * (j + 1))
+                nc.vector.tensor_tensor(total[:, cols], banks[j][:], fresh[:, cols], ADD)
+            return total
+
+        cc = relay(a, l1, l2, f1, b, "cc")
+        dd = relay(cc, l3, l4, f2, c, "dd")
+        y = look_up(dd, l5, "y")
+        nc.sync.dma_start(out[:, :HALF], y[:, :HALF])
+        nc.scalar.dma_start(out[:, HALF:], y[:, HALF:])

@@ -19,6 +19,7 @@ ADD = mybir.AluOpType.add
 P = 128
 BANK = 512
 HALF = I // 2
+TAIL = 320
 
 
 def tile_attend_relaythree_three_kernel(
@@ -40,23 +41,23 @@ def tile_attend_relaythree_three_kernel(
             nc.sync.dma_start(words[:].bitcast(I32), src.bitcast(I32))
             return words
 
-        def load_scales(src, name):
+        def load_scales(src, name, queue):
             plane = sb.tile([P, T], U8, name=name, align_bytes=64)
             for g in range(4):
-                nc.sync.dma_start(plane[32 * g : 32 * g + 4, :].bitcast(I32), src[0, 4 * g : 4 * g + 4, :].bitcast(I32))
+                queue.dma_start(plane[32 * g : 32 * g + 4, :].bitcast(I32), src[0, 4 * g : 4 * g + 4, :].bitcast(I32))
             return plane
 
         q_raw = sb.tile([P, 4, Q], F32, name="q_raw")
         nc.sync.dma_start(q_raw[:], query.rearrange("(p j) q -> p j q", j=4))
-        k_plane = load_scales(keys_scales, "k_plane")
+        k_plane = load_scales(keys_scales, "k_plane", nc.scalar)
         k_words = load_words(keys_words[0], 2 * T, "k_words")
         l1 = load_list(offs, "l1")
         l2 = load_list(offs2, "l2")
-        n_plane = load_scales(notes_scales, "n_plane")
+        n_plane = load_scales(notes_scales, "n_plane", nc.sync)
         n_words = load_words(notes_words[0].rearrange("p n t -> p (n t)"), 4 * T, "n_words")
         l3 = load_list(offs3, "l3")
         l4 = load_list(offs4, "l4")
-        u_plane = load_scales(users_scales, "u_plane")
+        u_plane = load_scales(users_scales, "u_plane", nc.sync)
         u_words = load_words(users_words[0], 2 * T, "u_words")
         l5 = load_list(offs5, "l5")
 
@@ -88,14 +89,16 @@ def tile_attend_relaythree_three_kernel(
             return acc
 
         a = sb.tile([P, T], F32, name="a")
-        for j in range(4):
-            acc = scores(k_words, k_plane, FP4X4, 2, 256 * j, 256, "a%d" % j)
+        c0 = 0
+        for j, n in enumerate((256, 256, 256, 128, 128)):
+            acc = scores(k_words, k_plane, FP4X4, 2, c0, n, "bank%d" % j)
             if j % 2 == 0:
-                nc.scalar.activation(a[:, 256 * j : 256 * (j + 1)], acc[:], COPY)
+                nc.scalar.activation(a[:, c0 : c0 + n], acc[:], COPY)
             else:
-                nc.vector.tensor_copy(a[:, 256 * j : 256 * (j + 1)], acc[:])
-        b = [scores(n_words, n_plane, FP8X4, 4, BANK * j, BANK, "b%d" % j) for j in range(2)]
-        c = [scores(u_words, u_plane, FP4X4, 2, BANK * j, BANK, "c%d" % j) for j in range(2)]
+                nc.vector.tensor_copy(a[:, c0 : c0 + n], acc[:])
+            c0 = c0 + n
+        b = [scores(n_words, n_plane, FP8X4, 4, BANK * j, BANK, "bank%d" % (5 + j)) for j in range(2)]
+        c = [scores(u_words, u_plane, FP4X4, 2, BANK * j, BANK, "bank%d" % (7 * (1 - j))) for j in range(2)]
 
         def look_up(window, lists, name):
             picked = sb.tile([P, I], F32, name=name)
@@ -107,9 +110,11 @@ def tile_attend_relaythree_three_kernel(
             picked = look_up(window, pick, name + "_picked")
             nc.vector.tensor_copy(fresh[:].indirect(place[:]), picked[:])
             total = sb.tile([P, T], F32, name=name)
-            for j in range(2):
-                cols = slice(BANK * j, BANK * (j + 1))
-                nc.vector.tensor_tensor(total[:, cols], banks[j][:], fresh[:, cols], ADD)
+            tail = sb.tile([P, TAIL], F32, name=name + "_tail")
+            nc.scalar.copy(tail[:], banks[1][:, BANK - TAIL :])
+            nc.vector.tensor_tensor(total[:, :BANK], banks[0][:], fresh[:, :BANK], ADD)
+            nc.vector.tensor_tensor(total[:, BANK : T - TAIL], banks[1][:, : BANK - TAIL], fresh[:, BANK : T - TAIL], ADD)
+            nc.gpsimd.tensor_tensor(total[:, T - TAIL :], tail[:], fresh[:, T - TAIL :], ADD)
             return total
 
         cc = relay(a, l1, l2, f1, b, "cc")

from contextlib import ExitStack

import concourse.mybir as mybir

D, T, I, Q = 512, 1024, 512, 128
FLOPS = 3 * 2 * D * T * Q

F32 = mybir.dt.float32
BF16 = mybir.dt.bfloat16
I32 = mybir.dt.int32
U32 = mybir.dt.uint32
U16 = mybir.dt.uint16
U8 = mybir.dt.uint8
FP8X4 = mybir.dt.float8_e4m3fn_x4
FP4X4 = mybir.dt.float4_e2m1fn_x4
COPY = mybir.ActivationFunctionType.Copy
ADD = mybir.AluOpType.add

P = 128
BANK = 512
HALF = I // 2
TAIL = 320


def tile_attend_relaythree_three_kernel(
    tc, query, keys_words, keys_scales, notes_words, notes_scales, users_words, users_scales,
    offs, offs2, offs3, offs4, offs5, out,
):
    nc = tc.nc
    with ExitStack() as ctx:
        sb = ctx.enter_context(tc.tile_pool(name="sb", bufs=1))
        ps = ctx.enter_context(tc.psum_pool(name="ps", bufs=1))

        def load_list(src, name):
            lists = sb.tile([P, I // 16], U16, name=name)
            nc.sync.dma_start(lists[:], src)
            return lists

        def load_words(src, nbytes, name):
            words = sb.tile([P, nbytes], U8, name=name, align_bytes=64)
            nc.sync.dma_start(words[:].bitcast(I32), src.bitcast(I32))
            return words

        def load_scales(src, name, queue):
            plane = sb.tile([P, T], U8, name=name, align_bytes=64)
            for g in range(4):
                queue.dma_start(plane[32 * g : 32 * g + 4, :].bitcast(I32), src[0, 4 * g : 4 * g + 4, :].bitcast(I32))
            return plane

        q_raw = sb.tile([P, 4, Q], F32, name="q_raw")
        nc.sync.dma_start(q_raw[:], query.rearrange("(p j) q -> p j q", j=4))
        k_plane = load_scales(keys_scales, "k_plane", nc.scalar)
        k_words = load_words(keys_words[0], 2 * T, "k_words")
        l1 = load_list(offs, "l1")
        l2 = load_list(offs2, "l2")
        n_plane = load_scales(notes_scales, "n_plane", nc.sync)
        n_words = load_words(notes_words[0].rearrange("p n t -> p (n t)"), 4 * T, "n_words")
        l3 = load_list(offs3, "l3")
        l4 = load_list(offs4, "l4")
        u_plane = load_scales(users_scales, "u_plane", nc.sync)
        u_words = load_words(users_words[0], 2 * T, "u_words")
        l5 = load_list(offs5, "l5")

        f1 = sb.tile([P, T], F32, name="f1")
        f2 = sb.tile([P, T], F32, name="f2")
        nc.vector.memset(f1[:], 0.0)
        nc.vector.memset(f2[:], 0.0)

        q_bf = sb.tile([P, Q, 4], BF16, name="q_bf", align_bytes=64)
        nc.vector.tensor_copy(
            q_bf[:].rearrange("p (c i) t -> p c t i", i=4),
            q_raw[:].rearrange("p t (c i) -> p c t i", i=4),
        )
        q_codes = sb.tile([P, Q], U32, name="q_codes", align_bytes=64)
        q_plane = sb.tile([P, Q], U8, name="q_plane", align_bytes=64)
        nc.vector.quantize_mx(q_codes[:].bitcast(FP8X4), q_plane[:], q_bf[:].rearrange("p c t -> p (c t)"))

        def scores(words, plane, dtype, per_col, c0, n, tag):
            acc = ps.tile([P, n], F32, name=tag)
            nc.tensor.matmul_mx(
                acc[:],
                lhsT=q_codes[:].bitcast(FP8X4),
                lhsT_scale=q_plane[:],
                rhs=words[:, per_col * c0 : per_col * (c0 + n)].bitcast(dtype),
                rhs_scale=plane[:, c0 : c0 + n],
                start=True,
                stop=True,
            )
            return acc

        a = sb.tile([P, T], F32, name="a")
        c0 = 0
        for j, n in enumerate((256, 256, 256, 128, 128)):
            acc = scores(k_words, k_plane, FP4X4, 2, c0, n, "bank%d" % j)
            if j % 2 == 0:
                nc.scalar.activation(a[:, c0 : c0 + n], acc[:], COPY)
            else:
                nc.vector.tensor_copy(a[:, c0 : c0 + n], acc[:])
            c0 = c0 + n
        b = [scores(n_words, n_plane, FP8X4, 4, BANK * j, BANK, "bank%d" % (5 + j)) for j in range(2)]
        c = [scores(u_words, u_plane, FP4X4, 2, BANK * j, BANK, "bank%d" % (7 * (1 - j))) for j in range(2)]

        def look_up(window, lists, name):
            picked = sb.tile([P, I], F32, name=name)
            nc.vector.tensor_copy(picked[:, :HALF], window[:].indirect(lists[:, : HALF // 16]))
            nc.scalar.activation(picked[:, HALF:], window[:].indirect(lists[:, HALF // 16 :]), COPY)
            return picked

        def relay(window, pick, place, fresh, banks, name):
            picked = look_up(window, pick, name + "_picked")
            nc.vector.tensor_copy(fresh[:].indirect(place[:]), picked[:])
            total = sb.tile([P, T], F32, name=name)
            tail = sb.tile([P, TAIL], F32, name=name + "_tail")
            nc.scalar.copy(tail[:], banks[1][:, BANK - TAIL :])
            nc.vector.tensor_tensor(total[:, :BANK], banks[0][:], fresh[:, :BANK], ADD)
            nc.vector.tensor_tensor(total[:, BANK : T - TAIL], banks[1][:, : BANK - TAIL], fresh[:, BANK : T - TAIL], ADD)
            nc.gpsimd.tensor_tensor(total[:, T - TAIL :], tail[:], fresh[:, T - TAIL :], ADD)
            return total

        cc = relay(a, l1, l2, f1, b, "cc")
        dd = relay(cc, l3, l4, f2, c, "dd")
        y = look_up(dd, l5, "y")
        nc.sync.dma_start(out[:, :HALF], y[:, :HALF])
        nc.scalar.dma_start(out[:, HALF:], y[:, HALF:])
